import numpy as np
import ml_dtypes

BF16 = ml_dtypes.bfloat16


def bf(x):
    return np.asarray(x, np.float32).astype(BF16)


def f32(x):
    return np.asarray(x, np.float32)


def f64(x):
    return np.asarray(x).astype(np.float64)


def striped(idx):
    return np.tile(idx.reshape(-1, 16).T, (8, 1))


S, K, M, N, D, V = 2048, 256, 512, 512, 2, 256


def setup_inputs():
    return {"table": bf(np.random.standard_normal((K, S))), "w": bf(np.random.standard_normal((D, K, M)) / np.sqrt(D * K)), "b": f32(0.5 * np.random.standard_normal((M, 1))), "offs": striped(np.random.permutation(np.tile(np.arange(S), 2))[:N])}


def reference(table, w, b, offs):
    idx = offs[:16].T.reshape(-1)
    x = f64(table)[:, idx]
    y = sum(f64(w)[t].T @ x[:, t * V : (t + 1) * V] for t in range(D))
    return y + f64(b)

@@ -1,0 +1,51 @@
+import concourse.mybir as mybir
+
+BF16, F32, U16 = mybir.dt.bfloat16, mybir.dt.float32, mybir.dt.uint16
+
+P = 128
+S = 2048
+K = 256
+M = 512
+ENDS = 2
+EDGES = 256
+KB = K // P
+MB = M // P
+COLS = EDGES // 16
+
+FLOPS = 2 * M * EDGES * ENDS * K
+
+
+def tile_gather_matmul_kernel(tc, table, w, b, offs, out):
+    nc = tc.nc
+    with (
+        tc.tile_pool(name="held", bufs=1) as held,
+        tc.tile_pool(name="staging", bufs=2) as staging,
+        tc.psum_pool(name="psum", bufs=2) as psum,
+    ):
+        offsets = held.tile([P, ENDS * COLS], U16, name="offsets")
+        nc.sync.dma_start(offsets[:], offs)
+
+        windows = [held.tile([P, S], BF16, name=f"window{kb}") for kb in range(KB)]
+        for kb in range(KB):
+            nc.sync.dma_start(windows[kb][:], table[kb * P : (kb + 1) * P, :])
+
+        weights = held.tile([P, ENDS * KB, M], BF16, name="weights")
+        nc.scalar.dma_start(weights[:], w.rearrange("t (kb p) m -> p (t kb) m", p=P))
+
+        bias = held.tile([P, MB], F32, name="bias")
+        nc.scalar.dma_start(bias[:], b.rearrange("(mb p) o -> p (mb o)", p=P))
+
+        for mb in range(MB):
+            bank = psum.tile([P, EDGES], F32, name="bank")
+            terms = [(t, kb) for t in range(ENDS) for kb in range(KB)]
+            for i, (t, kb) in enumerate(terms):
+                nc.tensor.matmul(
+                    bank[:],
+                    weights[:, t * KB + kb, mb * P : (mb + 1) * P],
+                    windows[kb][:].indirect(offsets[:, t * COLS : (t + 1) * COLS]),
+                    start=(i == 0),
+                    stop=(i == len(terms) - 1),
+                )
+            staged = staging.tile([P, EDGES], F32, name="staged")
+            nc.vector.tensor_scalar_add(staged[:], bank[:], bias[:, mb : mb + 1])
+            nc.sync.dma_start(out[mb * P : (mb + 1) * P, :], staged[:])

@@ -11,6 +11,8 @@ EDGES = 256
 KB = K // P
 MB = M // P
 COLS = EDGES // 16
+BANK = 512
+WARM_UPS = 4
 
 FLOPS = 2 * M * EDGES * ENDS * K
 
@@ -19,33 +21,56 @@ def tile_gather_matmul_kernel(tc, table, w, b, offs, out):
     nc = tc.nc
     with (
         tc.tile_pool(name="held", bufs=1) as held,
-        tc.tile_pool(name="staging", bufs=2) as staging,
-        tc.psum_pool(name="psum", bufs=2) as psum,
+        tc.psum_pool(name="psum", bufs=1) as psum,
     ):
         offsets = held.tile([P, ENDS * COLS], U16, name="offsets")
         nc.sync.dma_start(offsets[:], offs)
 
         windows = [held.tile([P, S], BF16, name=f"window{kb}") for kb in range(KB)]
-        for kb in range(KB):
-            nc.sync.dma_start(windows[kb][:], table[kb * P : (kb + 1) * P, :])
+        weights = [[held.tile([P, M], BF16, name=f"weights{kb}_{t}") for t in range(ENDS)] for kb in range(KB)]
 
-        weights = held.tile([P, ENDS * KB, M], BF16, name="weights")
-        nc.scalar.dma_start(weights[:], w.rearrange("t (kb p) m -> p (t kb) m", p=P))
+        def load_window(kb, split):
+            rows = slice(kb * P, (kb + 1) * P)
+            nc.sync.dma_start(windows[kb][:, :split], table[rows, :split])
+            nc.scalar.dma_start(windows[kb][:, split:], table[rows, split:])
+
+        def load_weights(queue, kb, t):
+            queue.dma_start(weights[kb][t][:], w[t, kb * P : (kb + 1) * P, :])
+
+        load_weights(nc.sync, 0, 0)
+        load_window(0, (S - M) // 2)
+        load_weights(nc.sync, 0, 1)
+        load_weights(nc.scalar, 1, 0)
+        load_weights(nc.sync, 1, 1)
+        load_window(1, S // 2)
 
         bias = held.tile([P, MB], F32, name="bias")
         nc.scalar.dma_start(bias[:], b.rearrange("(mb p) o -> p (mb o)", p=P))
 
+        zeros = held.tile([P, BANK], BF16, name="zeros")
+        nc.vector.memset(zeros[:], 0.0)
+        unread = psum.tile([P, BANK], F32, name="unread")
+        for warm_up in range(WARM_UPS):
+            nc.tensor.matmul(unread[:], zeros[:, :P], zeros[:], start=True, stop=True)
+
+        banks = [psum.tile([P, EDGES], F32, name=f"bank{mb}") for mb in range(MB)]
+        staged = [held.tile([P, EDGES], F32, name=f"staged{mb}") for mb in range(MB)]
+
+        def gathered_matmul(mb, kb, t):
+            nc.tensor.matmul(
+                banks[mb][:],
+                weights[kb][t][:, mb * P : (mb + 1) * P],
+                windows[kb][:].indirect(offsets[:, t * COLS : (t + 1) * COLS]),
+                start=(kb == 0 and t == 0),
+                stop=(kb == KB - 1 and t == ENDS - 1),
+            )
+
+        for t in range(ENDS):
+            for mb in range(MB):
+                gathered_matmul(mb, 0, t)
+        store_queues = [nc.sync, nc.scalar]
         for mb in range(MB):
-            bank = psum.tile([P, EDGES], F32, name="bank")
-            terms = [(t, kb) for t in range(ENDS) for kb in range(KB)]
-            for i, (t, kb) in enumerate(terms):
-                nc.tensor.matmul(
-                    bank[:],
-                    weights[:, t * KB + kb, mb * P : (mb + 1) * P],
-                    windows[kb][:].indirect(offsets[:, t * COLS : (t + 1) * COLS]),
-                    start=(i == 0),
-                    stop=(i == len(terms) - 1),
-                )
-            staged = staging.tile([P, EDGES], F32, name="staged")
-            nc.vector.tensor_scalar_add(staged[:], bank[:], bias[:, mb : mb + 1])
-            nc.sync.dma_start(out[mb * P : (mb + 1) * P, :], staged[:])
+            for t in range(ENDS):
+                gathered_matmul(mb, 1, t)
+            nc.vector.tensor_scalar_add(staged[mb][:], banks[mb][:], bias[:, mb : mb + 1])
+            store_queues[mb % 2].dma_start(out[mb * P : (mb + 1) * P, :], staged[mb][:])

@@ -11,8 +11,6 @@ EDGES = 256
 KB = K // P
 MB = M // P
 COLS = EDGES // 16
-BANK = 512
-WARM_UPS = 4
 
 FLOPS = 2 * M * EDGES * ENDS * K
 
@@ -46,12 +44,6 @@ def tile_gather_matmul_kernel(tc, table, w, b, offs, out):
 
         bias = held.tile([P, MB], F32, name="bias")
         nc.scalar.dma_start(bias[:], b.rearrange("(mb p) o -> p (mb o)", p=P))
-
-        zeros = held.tile([P, BANK], BF16, name="zeros")
-        nc.vector.memset(zeros[:], 0.0)
-        unread = psum.tile([P, BANK], F32, name="unread")
-        for warm_up in range(WARM_UPS):
-            nc.tensor.matmul(unread[:], zeros[:, :P], zeros[:], start=True, stop=True)
 
         banks = [psum.tile([P, EDGES], F32, name=f"bank{mb}") for mb in range(MB)]
         staged = [held.tile([P, EDGES], F32, name=f"staged{mb}") for mb in range(MB)]

@@ -24,26 +24,24 @@ def tile_gather_matmul_kernel(tc, table, w, b, offs, out):
         offsets = held.tile([P, ENDS * COLS], U16, name="offsets")
         nc.sync.dma_start(offsets[:], offs)
 
+        bias = held.tile([P, MB], F32, name="bias")
+        nc.scalar.dma_start(bias[:], b.rearrange("(mb p) o -> p (mb o)", p=P))
+
         windows = [held.tile([P, S], BF16, name=f"window{kb}") for kb in range(KB)]
         weights = [[held.tile([P, M], BF16, name=f"weights{kb}_{t}") for t in range(ENDS)] for kb in range(KB)]
 
-        def load_window(kb, split):
-            rows = slice(kb * P, (kb + 1) * P)
-            nc.sync.dma_start(windows[kb][:, :split], table[rows, :split])
-            nc.scalar.dma_start(windows[kb][:, split:], table[rows, split:])
+        def load_window(kb):
+            nc.sync.dma_start(windows[kb][:], table[kb * P : (kb + 1) * P, :])
 
-        def load_weights(queue, kb, t):
-            queue.dma_start(weights[kb][t][:], w[t, kb * P : (kb + 1) * P, :])
+        def load_weights(kb, t):
+            nc.sync.dma_start(weights[kb][t][:], w[t, kb * P : (kb + 1) * P, :])
 
-        load_weights(nc.sync, 0, 0)
-        load_window(0, (S - M) // 2)
-        load_weights(nc.sync, 0, 1)
-        load_weights(nc.scalar, 1, 0)
-        load_weights(nc.sync, 1, 1)
-        load_window(1, S // 2)
-
-        bias = held.tile([P, MB], F32, name="bias")
-        nc.scalar.dma_start(bias[:], b.rearrange("(mb p) o -> p (mb o)", p=P))
+        load_weights(0, 0)
+        load_window(0)
+        load_weights(0, 1)
+        load_weights(1, 0)
+        load_weights(1, 1)
+        load_window(1)
 
         banks = [psum.tile([P, EDGES], F32, name=f"bank{mb}") for mb in range(MB)]
         staged = [held.tile([P, EDGES], F32, name=f"staged{mb}") for mb in range(MB)]

@@ -22,10 +22,7 @@ def tile_gather_matmul_kernel(tc, table, w, b, offs, out):
         tc.psum_pool(name="psum", bufs=1) as psum,
     ):
         offsets = held.tile([P, ENDS * COLS], U16, name="offsets")
-        nc.sync.dma_start(offsets[:], offs)
-
         bias = held.tile([P, MB], F32, name="bias")
-        nc.scalar.dma_start(bias[:], b.rearrange("(mb p) o -> p (mb o)", p=P))
 
         windows = [held.tile([P, S], BF16, name=f"window{kb}") for kb in range(KB)]
         weights = [[held.tile([P, M], BF16, name=f"weights{kb}_{t}") for t in range(ENDS)] for kb in range(KB)]
@@ -33,15 +30,18 @@ def tile_gather_matmul_kernel(tc, table, w, b, offs, out):
         def load_window(kb):
             nc.sync.dma_start(windows[kb][:], table[kb * P : (kb + 1) * P, :])
 
-        def load_weights(kb, t):
-            nc.sync.dma_start(weights[kb][t][:], w[t, kb * P : (kb + 1) * P, :])
+        def load_weights(kb, t, first=0, last=M):
+            nc.sync.dma_start(weights[kb][t][:, first:last], w[t, kb * P : (kb + 1) * P, first:last])
 
-        load_weights(0, 0)
         load_window(0)
+        load_weights(0, 0, 0, M // 2)
+        nc.sync.dma_start(offsets[:], offs)
+        load_weights(0, 0, M // 2, M)
         load_weights(0, 1)
         load_weights(1, 0)
         load_weights(1, 1)
         load_window(1)
+        nc.sync.dma_start(bias[:], b.rearrange("(mb p) o -> p (mb o)", p=P))
 
         banks = [psum.tile([P, EDGES], F32, name=f"bank{mb}") for mb in range(MB)]
         staged = [held.tile([P, EDGES], F32, name=f"staged{mb}") for mb in range(MB)]

@@ -38,9 +38,11 @@ def tile_gather_matmul_kernel(tc, table, w, b, offs, out):
         nc.sync.dma_start(offsets[:], offs)
         load_weights(0, 0, M // 2, M)
         load_weights(0, 1)
-        load_weights(1, 0)
-        load_weights(1, 1)
+        load_weights(1, 0, 0, M // 2)
+        load_weights(1, 1, 0, M // 2)
         load_window(1)
+        load_weights(1, 0, M // 2, M)
+        load_weights(1, 1, M // 2, M)
         nc.sync.dma_start(bias[:], b.rearrange("(mb p) o -> p (mb o)", p=P))
 
         banks = [psum.tile([P, EDGES], F32, name=f"bank{mb}") for mb in range(MB)]

@@ -60,7 +60,7 @@ def tile_gather_matmul_kernel(tc, table, w, b, offs, out):
         for t in range(ENDS):
             for mb in range(MB):
                 gathered_matmul(mb, 0, t)
-        store_queues = [nc.sync, nc.scalar]
+        store_queues = [nc.scalar, nc.sync]
         for mb in range(MB):
             for t in range(ENDS):
                 gathered_matmul(mb, 1, t)

@@ -60,9 +60,8 @@ def tile_gather_matmul_kernel(tc, table, w, b, offs, out):
         for t in range(ENDS):
             for mb in range(MB):
                 gathered_matmul(mb, 0, t)
-        store_queues = [nc.scalar, nc.sync]
         for mb in range(MB):
             for t in range(ENDS):
                 gathered_matmul(mb, 1, t)
             nc.vector.tensor_scalar_add(staged[mb][:], banks[mb][:], bias[:, mb : mb + 1])
-            store_queues[mb % 2].dma_start(out[mb * P : (mb + 1) * P, :], staged[mb][:])
+            nc.sync.dma_start(out[mb * P : (mb + 1) * P, :], staged[mb][:])

@@ -60,8 +60,15 @@ def tile_gather_matmul_kernel(tc, table, w, b, offs, out):
         for t in range(ENDS):
             for mb in range(MB):
                 gathered_matmul(mb, 0, t)
+        def finish(mb, pieces):
+            run = EDGES // pieces
+            for first in range(0, EDGES, run):
+                nc.vector.tensor_scalar_add(
+                    staged[mb][:, first : first + run], banks[mb][:, first : first + run], bias[:, mb : mb + 1]
+                )
+                nc.sync.dma_start(out[mb * P : (mb + 1) * P, first : first + run], staged[mb][:, first : first + run])
+
         for mb in range(MB):
             for t in range(ENDS):
                 gathered_matmul(mb, 1, t)
-            nc.vector.tensor_scalar_add(staged[mb][:], banks[mb][:], bias[:, mb : mb + 1])
-            nc.sync.dma_start(out[mb * P : (mb + 1) * P, :], staged[mb][:])
+            finish(mb, pieces=2 if mb == MB - 1 else 1)

@@ -25,24 +25,28 @@ def tile_gather_matmul_kernel(tc, table, w, b, offs, out):
         bias = held.tile([P, MB], F32, name="bias")
 
         windows = [held.tile([P, S], BF16, name=f"window{kb}") for kb in range(KB)]
-        weights = [[held.tile([P, M], BF16, name=f"weights{kb}_{t}") for t in range(ENDS)] for kb in range(KB)]
+        weights = [held.tile([P, ENDS, M], BF16, name=f"weights{kb}") for kb in range(KB)]
 
         def load_window(kb):
             nc.sync.dma_start(windows[kb][:], table[kb * P : (kb + 1) * P, :])
 
-        def load_weights(kb, t, first=0, last=M):
-            nc.sync.dma_start(weights[kb][t][:, first:last], w[t, kb * P : (kb + 1) * P, first:last])
+        def load_weights(kb, ends, first=0, last=M):
+            nc.sync.dma_start(
+                weights[kb][:, ends, first:last],
+                w[ends, kb * P : (kb + 1) * P, first:last].rearrange("t k m -> k t m"),
+            )
+
+        one_end = [slice(t, t + 1) for t in range(ENDS)]
+        both_ends = slice(0, ENDS)
 
         load_window(0)
-        load_weights(0, 0, 0, M // 2)
+        load_weights(0, one_end[0], 0, M // 2)
         nc.sync.dma_start(offsets[:], offs)
-        load_weights(0, 0, M // 2, M)
-        load_weights(0, 1)
-        load_weights(1, 0, 0, M // 2)
-        load_weights(1, 1, 0, M // 2)
+        load_weights(0, one_end[0], M // 2, M)
+        load_weights(0, one_end[1])
+        load_weights(1, both_ends, 0, M // 2)
         load_window(1)
-        load_weights(1, 0, M // 2, M)
-        load_weights(1, 1, M // 2, M)
+        load_weights(1, both_ends, M // 2, M)
         nc.sync.dma_start(bias[:], b.rearrange("(mb p) o -> p (mb o)", p=P))
 
         banks = [psum.tile([P, EDGES], F32, name=f"bank{mb}") for mb in range(MB)]
@@ -51,7 +55,7 @@ def tile_gather_matmul_kernel(tc, table, w, b, offs, out):
         def gathered_matmul(mb, kb, t):
             nc.tensor.matmul(
                 banks[mb][:],
-                weights[kb][t][:, mb * P : (mb + 1) * P],
+                weights[kb][:, t, mb * P : (mb + 1) * P],
                 windows[kb][:].indirect(offsets[:, t * COLS : (t + 1) * COLS]),
                 start=(kb == 0 and t == 0),
                 stop=(kb == KB - 1 and t == ENDS - 1),

@@ -40,13 +40,13 @@ def tile_gather_matmul_kernel(tc, table, w, b, offs, out):
         both_ends = slice(0, ENDS)
 
         load_window(0)
-        load_weights(0, one_end[0], 0, M // 2)
+        load_weights(0, one_end[0], 0, P)
         nc.sync.dma_start(offsets[:], offs)
-        load_weights(0, one_end[0], M // 2, M)
+        load_weights(0, one_end[0], P, M)
         load_weights(0, one_end[1])
-        load_weights(1, both_ends, 0, M // 2)
+        load_weights(1, both_ends, 0, P)
         load_window(1)
-        load_weights(1, both_ends, M // 2, M)
+        load_weights(1, both_ends, P, M)
         nc.sync.dma_start(bias[:], b.rearrange("(mb p) o -> p (mb o)", p=P))
 
         banks = [psum.tile([P, EDGES], F32, name=f"bank{mb}") for mb in range(MB)]

@@ -44,9 +44,11 @@ def tile_gather_matmul_kernel(tc, table, w, b, offs, out):
         nc.sync.dma_start(offsets[:], offs)
         load_weights(0, one_end[0], P, M)
         load_weights(0, one_end[1])
-        load_weights(1, both_ends, 0, P)
+        load_weights(1, one_end[0], 0, P)
         load_window(1)
-        load_weights(1, both_ends, P, M)
+        load_weights(1, one_end[1], 0, P)
+        load_weights(1, both_ends, P, 2 * P)
+        load_weights(1, both_ends, 2 * P, M)
         nc.sync.dma_start(bias[:], b.rearrange("(mb p) o -> p (mb o)", p=P))
 
         banks = [psum.tile([P, EDGES], F32, name=f"bank{mb}") for mb in range(MB)]

@@ -48,8 +48,8 @@ def tile_gather_matmul_kernel(tc, table, w, b, offs, out):
         load_window(1)
         load_weights(1, one_end[1], 0, P)
         load_weights(1, both_ends, P, 2 * P)
-        load_weights(1, both_ends, 2 * P, M)
         nc.sync.dma_start(bias[:], b.rearrange("(mb p) o -> p (mb o)", p=P))
+        load_weights(1, both_ends, 2 * P, M)
 
         banks = [psum.tile([P, EDGES], F32, name=f"bank{mb}") for mb in range(MB)]
         staged = [held.tile([P, EDGES], F32, name=f"staged{mb}") for mb in range(MB)]

import concourse.mybir as mybir

BF16, F32, U16 = mybir.dt.bfloat16, mybir.dt.float32, mybir.dt.uint16

P = 128
S = 2048
K = 256
M = 512
ENDS = 2
EDGES = 256
KB = K // P
MB = M // P
COLS = EDGES // 16

FLOPS = 2 * M * EDGES * ENDS * K


def tile_gather_matmul_kernel(tc, table, w, b, offs, out):
    nc = tc.nc
    with (
        tc.tile_pool(name="held", bufs=1) as held,
        tc.psum_pool(name="psum", bufs=1) as psum,
    ):
        offsets = held.tile([P, ENDS * COLS], U16, name="offsets")
        bias = held.tile([P, MB], F32, name="bias")

        windows = [held.tile([P, S], BF16, name=f"window{kb}") for kb in range(KB)]
        weights = [held.tile([P, ENDS, M], BF16, name=f"weights{kb}") for kb in range(KB)]

        def load_window(kb):
            nc.sync.dma_start(windows[kb][:], table[kb * P : (kb + 1) * P, :])

        def load_weights(kb, ends, first=0, last=M):
            nc.sync.dma_start(
                weights[kb][:, ends, first:last],
                w[ends, kb * P : (kb + 1) * P, first:last].rearrange("t k m -> k t m"),
            )

        one_end = [slice(t, t + 1) for t in range(ENDS)]
        both_ends = slice(0, ENDS)

        load_window(0)
        load_weights(0, one_end[0], 0, P)
        nc.sync.dma_start(offsets[:], offs)
        load_weights(0, one_end[0], P, M)
        load_weights(0, one_end[1])
        load_weights(1, one_end[0], 0, P)
        load_window(1)
        load_weights(1, one_end[1], 0, P)
        load_weights(1, both_ends, P, 2 * P)
        nc.sync.dma_start(bias[:], b.rearrange("(mb p) o -> p (mb o)", p=P))
        load_weights(1, both_ends, 2 * P, M)

        banks = [psum.tile([P, EDGES], F32, name=f"bank{mb}") for mb in range(MB)]
        staged = [held.tile([P, EDGES], F32, name=f"staged{mb}") for mb in range(MB)]

        def gathered_matmul(mb, kb, t):
            nc.tensor.matmul(
                banks[mb][:],
                weights[kb][:, t, mb * P : (mb + 1) * P],
                windows[kb][:].indirect(offsets[:, t * COLS : (t + 1) * COLS]),
                start=(kb == 0 and t == 0),
                stop=(kb == KB - 1 and t == ENDS - 1),
            )

        for t in range(ENDS):
            for mb in range(MB):
                gathered_matmul(mb, 0, t)
        def finish(mb, pieces):
            run = EDGES // pieces
            for first in range(0, EDGES, run):
                nc.vector.tensor_scalar_add(
                    staged[mb][:, first : first + run], banks[mb][:, first : first + run], bias[:, mb : mb + 1]
                )
                nc.sync.dma_start(out[mb * P : (mb + 1) * P, first : first + run], staged[mb][:, first : first + run])

        for mb in range(MB):
            for t in range(ENDS):
                gathered_matmul(mb, 1, t)
            finish(mb, pieces=2 if mb == MB - 1 else 1)
